import numpy as np
import ml_dtypes


def mxq(x, axis, fmt="e4m3"):
    dtype, down = {"e4m3": (ml_dtypes.float8_e4m3fn, 7), "e5m2": (ml_dtypes.float8_e5m2, 14)}[fmt]
    v = np.moveaxis(np.asarray(x, np.float32).astype(ml_dtypes.bfloat16).astype(np.float64), axis, -1)
    blocks = v.reshape(v.shape[:-1] + (-1, 32))
    amax = np.abs(blocks).max(-1, keepdims=True)
    byte = np.maximum(np.where(amax > 0, np.frexp(amax)[1] - 1 + 127, 0) - down, 1)
    scale = np.exp2(byte - 127.0)
    codes = (blocks / scale).astype(np.float32).astype(dtype).astype(np.float64)
    return np.moveaxis((codes * scale).reshape(v.shape), -1, axis)


WIDE = False


def mx_kscale(k):
    if not WIDE:
        return np.ones(k)
    levels = np.array([10, -10, 5, -5, 0])
    if k % 512:
        return np.exp2(np.random.permutation(np.resize(levels, k // 32))).repeat(32)
    a = np.empty((k // 512, 16))
    for p in range(k // 512):
        a[p, :8] = np.random.permutation(np.resize(levels, 8))
        for g in range(8):
            far = levels[np.abs(levels - a[p, g]) >= 10]
            a[p, g + 8] = far[np.random.randint(len(far))]
    return np.exp2(a.ravel()).repeat(32)


def f64(x):
    return np.asarray(x).astype(np.float64)


def striped(idx):
    return np.tile(idx.reshape(-1, 16).T, (8, 1)).astype(np.uint16)


def unstriped(offs):
    return offs[:16].T.reshape(-1).astype(np.int64)


def striped8(idx):
    return np.concatenate([x.reshape(-1, 16).T for x in idx]).astype(np.uint16)


def runs(offs, k):
    lists = np.stack([offs[16 * r : 16 * r + 16].T.reshape(-1) for r in range(8)]).astype(np.int64)
    return lists[np.arange(k) % 512 // 64]


def pack_weight(w):
    k, n = w.shape
    w = f64(np.asarray(w, np.float32).astype(ml_dtypes.bfloat16)).reshape(k // 32, 32, n)
    amax = np.abs(w).max(1)
    byte = np.clip(np.where(amax > 0, np.frexp(amax)[1] - 1 + 127 - 7, 1), 1, 254)
    scaled = (w * np.exp2(127.0 - byte)[:, None, :]).reshape(k, n).astype(np.float32)
    words = np.ascontiguousarray(scaled.reshape(k // 512, 128, 4, n).transpose(0, 1, 3, 2)).astype(ml_dtypes.float8_e4m3fn).view(np.uint8)
    return words, np.ascontiguousarray(byte.astype(np.uint8).reshape(k // 512, 16, n))


def unpack_weight(words, scales):
    g, p, n, _ = words.shape
    vals = np.ascontiguousarray(words).view(ml_dtypes.float8_e4m3fn).astype(np.float64) * np.repeat(np.exp2(scales.astype(np.float64) - 127.0), 8, axis=1)[..., None]
    return vals.transpose(0, 1, 3, 2).reshape(g * 512, n)


E2M1 = np.array([0.0, 0.5, 1.0, 1.5, 2.0, 3.0, 4.0, 6.0, -0.0, -0.5, -1.0, -1.5, -2.0, -3.0, -4.0, -6.0])


def pack_fp4(w):
    k, n = w.shape
    w = f64(np.asarray(w, np.float32).astype(ml_dtypes.bfloat16)).reshape(k // 32, 32, n)
    amax = np.abs(w).max(1)
    mant, ex = np.frexp(amax / 6.0)
    byte = np.clip(np.where(amax > 0, np.where(mant > 0.5, ex, ex - 1) + 127, 1), 1, 254)
    scaled = (w * np.exp2(127.0 - byte)[:, None, :]).reshape(k, n).astype(np.float32)
    c = np.ascontiguousarray(scaled.reshape(k // 512, 128, 4, n).transpose(0, 1, 3, 2)).astype(ml_dtypes.float4_e2m1fn).view(np.uint8) & 0xF
    words = (c[..., 0::2] | (c[..., 1::2] << 4)).reshape(k // 512, 128, 2 * n)
    return np.ascontiguousarray(words), np.ascontiguousarray(byte.astype(np.uint8).reshape(k // 512, 16, n))


def unpack_fp4(words, scales):
    g, _, n = scales.shape
    words = np.ascontiguousarray(words).reshape(g, 128, n, 2)
    nib = np.empty((g, 128, n, 4), np.uint8)
    nib[..., 0::2] = words & 0xF
    nib[..., 1::2] = words >> 4
    vals = E2M1[nib] * np.repeat(np.exp2(scales.astype(np.float64) - 127.0), 8, axis=1)[..., None]
    return vals.transpose(0, 1, 3, 2).reshape(g * 512, n)


def sigmoid(v):
    return 1.0 / (1.0 + np.exp(-np.maximum(v, -700.0)))

def planes(y):
    n, m = y.shape
    v = y.astype(np.float32).astype(ml_dtypes.bfloat16).astype(np.float64).reshape(n // 32, 32, m)
    top = np.abs(v).max(1)
    byte = np.clip(np.where(top > 0, np.frexp(top)[1] - 1 + 127 - 7, 1), 1, 254)
    codes = (v * np.exp2(127.0 - byte)[:, None, :]).reshape(n, m).astype(np.float32).astype(ml_dtypes.float8_e4m3fn).view(np.uint8)
    words = codes.reshape(n // 512, 128, 4, m).transpose(0, 1, 3, 2)
    return np.ascontiguousarray(words), np.ascontiguousarray(byte.astype(np.uint8).reshape(n // 512, 16, m))


K, T, S, V, H, W = 512, 2048, 512, 512, 512, 256


def setup_inputs():
    n = np.random.standard_normal
    s = mx_kscale(K)[:, None]
    u = mx_kscale(S)
    packed_xT = pack_weight(n((K, T)) * s)
    packed_w1 = pack_fp4(n((K, H)) / np.sqrt(K) / s)
    packed_w2 = pack_fp4(n((K, H)) / np.sqrt(K) / s)
    perm = np.stack([np.random.permutation(V) for _ in range(8)])
    return {
        "x_words": packed_xT[0],
        "x_scales": packed_xT[1],
        "w1_words": packed_w1[0],
        "w1_scales": packed_w1[1],
        "w2_words": packed_w2[0],
        "w2_scales": packed_w2[1],
        "ga": (np.random.uniform(0.5, 1.5, (H, 1)) * u[:, None]).astype(np.float32),
        "gb": (np.random.uniform(0.5, 1.5, (H, 1)) / u[:, None]).astype(np.float32),
        "offs": striped(np.random.permutation(T)[:S]),
        "two": striped(np.random.permutation(T)[:V]),
        "n1": striped8(np.stack([np.random.permutation(S) for _ in range(8)])),
        "n2": striped8(np.stack([np.random.permutation(V) for _ in range(8)])),
        "n3": striped8(np.stack([np.random.permutation(V) for _ in range(8)])),
        "n4": striped8(perm[:, :W]),
        "n5": striped8(perm[:, W:]),
    }


def reference(x_words, x_scales, w1_words, w1_scales, w2_words, w2_scales, ga, gb, offs, two, n1, n2, n3, n4, n5):
    xq = unpack_weight(x_words, x_scales)[:, unstriped(offs)]
    a = unpack_fp4(w1_words, w1_scales).T @ xq
    st = a * (sigmoid(a[np.arange(H)[:, None], runs(n1, H)]))
    z = f64(ga) * (np.maximum(st, st[np.arange(H)[:, None], runs(n1, H)]))
    x_two = unpack_weight(x_words, x_scales)[:, unstriped(two)]
    b = unpack_fp4(w2_words, w2_scales).T @ x_two
    st2 = b + 0.5 * (b[np.arange(H)[:, None], runs(n2, H)])
    z2 = f64(gb) * (st2 - (st2[np.arange(H)[:, None], runs(n3, H)]))
    s = 0.0625 * ((mxq(z, 0, "e4m3").T @ mxq(z2, 0, "e4m3")))
    pa = s[np.arange(S)[:, None], runs(n4, S)]
    pb = s[np.arange(S)[:, None], runs(n5, S)]
    rb = np.minimum(pa, pb)
    ra = np.maximum(pa, pb)
    ds = np.zeros((S, V))
    ds[np.arange(S)[:, None], runs(n4, S)] = ra
    out = ds.copy()
    out[np.arange(S)[:, None], runs(n5, S)] = rb
    return (out,) + planes(out)

@@ -1,0 +1,247 @@
+from contextlib import ExitStack
+
+import concourse.mybir as mybir
+
+F32 = mybir.dt.float32
+BF16 = mybir.dt.bfloat16
+I32 = mybir.dt.int32
+U32 = mybir.dt.uint32
+U16 = mybir.dt.uint16
+U8 = mybir.dt.uint8
+FP8X4 = mybir.dt.float8_e4m3fn_x4
+FP4X4 = mybir.dt.float4_e2m1fn_x4
+ALU = mybir.AluOpType
+ACT = mybir.ActivationFunctionType
+
+P = 128
+T = 2048
+N = 512
+HALF = 256
+WIN = 1024
+FLOPS = 3 * 2 * 512 * 512 * 512
+
+
+def tile_picked_kqtwicphoporder_none_po_kernel(
+    tc, x_words, x_scales, w1_words, w1_scales, w2_words, w2_scales, ga, gb, offs, two, n1, n2, n3, n4, n5, out_0, out_1, out_2
+):
+    nc = tc.nc
+    with ExitStack() as ctx:
+        keep = ctx.enter_context(tc.tile_pool(name="keep", bufs=1))
+        psum = ctx.enter_context(tc.psum_pool(name="psum", bufs=1))
+
+        def sb(name, shape, dtype, tag=None):
+            return keep.tile(shape, dtype, name=name, tag=tag or name, align_bytes=64)
+
+        def load_list(name, src):
+            lst = keep.tile(list(src.shape), U16, name=name)
+            nc.sync.dma_start(lst[:], src)
+            return lst
+
+        def load_scale_rows(tile, src, queue):
+            for q in range(4):
+                queue.dma_start(tile[32 * q : 32 * q + 4, :].bitcast(I32), src[0, 4 * q : 4 * q + 4, :].bitcast(I32))
+
+        xs = sb("xs", [P, T], U8)
+        w2s_raw = sb("w2s_raw", [P, N], U8)
+        w1s_raw = sb("w1s_raw", [P, N], U8)
+        warm = sb("warm", [P, 8], F32)
+        warm_out = sb("warm_out", [P, 8], F32)
+        nc.gpsimd.memset(xs[:].bitcast(I32), 0)
+        nc.vector.memset(w2s_raw[:].bitcast(I32), 0)
+        nc.vector.memset(warm[:], 0.0)
+        nc.vector.memset(w1s_raw[:].bitcast(I32), 0)
+        gains = sb("gains", [P, 16], F32)
+        nc.gpsimd.dma_start(gains[:, 0:4], ga.rearrange("(p t) o -> p (t o)", t=4))
+        nc.gpsimd.dma_start(gains[:, 8:12], gb.rearrange("(p t) o -> p (t o)", t=4))
+
+        xw = sb("xw", [P, T], I32)
+        w2w_raw = sb("w2w_raw", [P, 2 * N], U8)
+        w1w_raw = sb("w1w_raw", [P, 2 * N], U8)
+        l_two = load_list("l_two", two)
+        nc.scalar.dma_start(w2w_raw[:].bitcast(I32), w2_words[0].bitcast(I32))
+        nc.sync.dma_start(xw[:], x_words[0].rearrange("p n r -> p (n r)").bitcast(I32))
+        load_scale_rows(xs, x_scales, nc.sync)
+        load_scale_rows(w2s_raw, w2_scales, nc.sync)
+        nc.scalar.activation(warm_out[:], warm[:], ACT.Sigmoid)
+        l_offs = load_list("l_offs", offs)
+        l_n2 = load_list("l_n2", n2)
+        nc.sync.dma_start(w1w_raw[:].bitcast(I32), w1_words[0].bitcast(I32))
+        load_scale_rows(w1s_raw, w1_scales, nc.sync)
+        l_n1 = load_list("l_n1", n1)
+        l_n3 = load_list("l_n3", n3)
+        l_n5 = load_list("l_n5", n5)
+        l_n4 = load_list("l_n4", n4)
+
+        step = sb("step", [P, 4], F32)
+        sign = sb("sign", [P, 4], F32)
+        ga_abs = sb("ga_abs", [P, 4], F32)
+        gb_signed = sb("gb_signed", [P, 4], F32)
+        gb_full = sb("gb_full", [P, 4], F32)
+        gb_half = sb("gb_half", [P, 4], F32)
+        nc.gpsimd.tensor_scalar(step[:], gains[:, 0:4], 0.0, 2.0, ALU.is_ge, ALU.mult)
+        nc.gpsimd.tensor_scalar(sign[:], step[:], 1.0, -1.0, ALU.mult, ALU.add)
+        nc.gpsimd.tensor_tensor(gb_signed[:], gains[:, 8:12], sign[:], ALU.mult)
+        nc.gpsimd.tensor_scalar(gb_half[:], gb_signed[:], -0.5, 0.0, ALU.mult, ALU.add)
+        nc.gpsimd.tensor_scalar(gb_full[:], gb_signed[:], -1.0, 0.0, ALU.mult, ALU.add)
+        nc.gpsimd.tensor_tensor(ga_abs[:], gains[:, 0:4], sign[:], ALU.mult)
+
+        def deal(name, raw, width, run):
+            dealt = sb(name, [P, width], U8)
+            nc.vector.tensor_copy(
+                dealt[:].rearrange("p (t m r) -> p m t r", t=4, r=run),
+                raw[:].rearrange("p (m t r) -> p m t r", t=4, r=run),
+            )
+            return dealt
+
+        xs_two = sb("xs_two", [P, N], U8)
+        xs_offs = sb("xs_offs", [P, N], U8)
+        xw_two = sb("xw_two", [P, N], U32)
+        w2w = deal("w2w", w2w_raw, 2 * N, 2)
+        nc.vector.tensor_copy(xs_two[:], xs[:].indirect(l_two[:]))
+        nc.vector.tensor_copy(xw_two[:], xw[:].bitcast(U32).indirect(l_two[:]))
+        w2s = deal("w2s", w2s_raw, N, 1)
+        nc.vector.tensor_copy(xs_offs[:], xs[:].indirect(l_offs[:]))
+        xw_offs = sb("xw_offs", [P, N], U32, tag="w2s_raw")
+        nc.vector.tensor_copy(xw_offs[:], xw[:].bitcast(U32).indirect(l_offs[:]))
+        w1w = deal("w1w", w1w_raw, 2 * N, 2)
+        w1s = deal("w1s", w1s_raw, N, 1)
+
+        def project(tag, ww, ws, words, scales, t):
+            acc = psum.tile([P, N], F32, name=tag, tag=tag)
+            nc.tensor.matmul_mx(
+                out=acc[:],
+                lhsT=ww[:, 2 * P * t : 2 * P * (t + 1)].bitcast(FP4X4),
+                lhsT_scale=ws[:, P * t : P * (t + 1)],
+                rhs=words[:].bitcast(FP8X4),
+                rhs_scale=scales[:],
+                start=True,
+                stop=True,
+            )
+            return acc
+
+        b_ps = [project("b%d" % t, w2w, w2s, xw_two, xs_two, t) for t in range(4)]
+        a_ps = [project("a%d" % t, w1w, w1s, xw_offs, xs_offs, t) for t in range(4)]
+        st2 = []
+        st2_copy = []
+        for t in range(4):
+            half_win = sb("half_win%d" % t, [P, WIN], F32)
+            b_full = sb("b_full%d" % t, [P, N], F32)
+            nc.scalar.activation(half_win[:, 0:N], b_ps[t][:], ACT.Copy, scale=gb_half[:, t : t + 1])
+            nc.scalar.activation(b_full[:], b_ps[t][:], ACT.Copy, scale=gb_full[:, t : t + 1])
+            win = sb("st2_%d" % t, [P, WIN], F32)
+            nc.vector.tensor_tensor(win[:, 0:N], half_win[:].indirect(l_n2[:]), b_full[:], ALU.add)
+            cp = sb("st2_copy%d" % t, [P, N], F32)
+            nc.sync.dma_start(cp[:], win[:, 0:N])
+            st2.append(win)
+            st2_copy.append(cp)
+        sig = []
+        for t in range(4):
+            a_win = sb("a_win%d" % t, [P, WIN], F32)
+            nc.scalar.copy(a_win[:, 0:N], a_ps[t][:])
+            sg = sb("sig%d" % t, [P, N], F32)
+            nc.scalar.activation(sg[:], a_win[:].indirect(l_n1[:]), ACT.Sigmoid)
+            sig.append(sg)
+        z2 = sb("z2", [P, 4, N], F32)
+        for t in range(4):
+            nc.vector.tensor_tensor(z2[:, t, :], st2[t][:].indirect(l_n3[:]), st2_copy[t][:], ALU.subtract)
+        z2_in = sb("z2_in", [P, N, 4], BF16)
+        nc.scalar.copy(z2_in[:], z2[:].rearrange("p t c -> p c t"))
+
+        st = [sb("st%d" % t, [P, WIN], F32) for t in range(4)]
+        st_n1 = [sb("st_n1_%d" % t, [P, N], F32) for t in range(4)]
+        z = sb("z", [P, 4, N], BF16)
+
+        def gate(t):
+            nc.vector.scalar_tensor_tensor(st[t][:, 0:N], a_ps[t][:], ga_abs[:, t : t + 1], sig[t][:], ALU.mult, ALU.mult)
+
+        def fetch(t):
+            nc.vector.tensor_copy(st_n1[t][:], st[t][:].indirect(l_n1[:]))
+
+        def larger(t):
+            nc.vector.tensor_tensor(z[:, t, :], st[t][:, 0:N], st_n1[t][:], ALU.max)
+
+        for stage in (gate, fetch):
+            for t in range(4):
+                stage(t)
+        z2_w = sb("z2_w", [P, N], U32)
+        z2_s = sb("z2_s", [P, N], U8)
+        nc.vector.quantize_mx(out=z2_w[:].bitcast(FP8X4), scales=z2_s[:], in_=z2_in[:].rearrange("p c t -> p (c t)"))
+        for t in range(4):
+            larger(t)
+
+        z_in = [sb("z_in%d" % u, [P, P, 4], BF16) for u in range(4)]
+        z_w = [sb("z_w%d" % u, [P, P], U32) for u in range(4)]
+        z_s = [sb("z_s%d" % u, [P, P], U8) for u in range(4)]
+        s_win = [sb("s_win%d" % u, [P, N], F32) for u in range(4)]
+
+        def weave(u):
+            nc.vector.tensor_copy(z_in[u][:], z[:].rearrange("p t (m u) -> p u m t", u=4)[:, u])
+
+        def product(u):
+            nc.vector.quantize_mx(out=z_w[u][:].bitcast(FP8X4), scales=z_s[u][:], in_=z_in[u][:].rearrange("p m t -> p (m t)"))
+            acc = psum.tile([P, N], F32, name="s%d" % u, tag="b%d" % u)
+            nc.tensor.matmul_mx(
+                out=acc[:], lhsT=z_w[u][:].bitcast(FP8X4), lhsT_scale=z_s[u][:], rhs=z2_w[:].bitcast(FP8X4), rhs_scale=z2_s[:], start=True, stop=True
+            )
+            nc.scalar.activation(s_win[u][:], acc[:], ACT.Copy, scale=0.0625)
+
+        weave(0)
+        for u in range(4):
+            if u + 1 < 4:
+                weave(u + 1)
+            product(u)
+
+        pb = [sb("pb%d" % u, [P, HALF], F32) for u in range(4)]
+        diff = [sb("diff%d" % u, [P, HALF], F32) for u in range(4)]
+        up = [sb("up%d" % u, [P, HALF], F32) for u in range(4)]
+        down_abs = [sb("down_abs%d" % u, [P, HALF], F32) for u in range(4)]
+        down = [sb("down%d" % u, [P, HALF], F32) for u in range(4)]
+        res = [sb("res%d" % u, [P, N], F32) for u in range(4)]
+        out_in = sb("out_in", [P, N, 4], BF16)
+        out_rows = out_0.rearrange("(p u) v -> p u v", u=4)
+
+        def fetch_b(u):
+            nc.vector.tensor_copy(pb[u][:], s_win[u][:].indirect(l_n5[:]))
+
+        def fetch_diff(u):
+            nc.vector.tensor_tensor(diff[u][:], s_win[u][:].indirect(l_n4[:]), pb[u][:], ALU.subtract)
+            nc.scalar.activation(up[u][:], diff[u][:], ACT.Relu)
+            nc.scalar.activation(down_abs[u][:], diff[u][:], ACT.Relu, scale=-1.0)
+            nc.scalar.activation(down[u][:], down_abs[u][:], ACT.Copy, scale=-1.0)
+
+        def put_larger(u):
+            nc.vector.tensor_tensor(res[u][:].indirect(l_n4[:]), pb[u][:], up[u][:], ALU.add)
+
+        def put_smaller(u):
+            nc.vector.tensor_tensor(res[u][:].indirect(l_n5[:]), pb[u][:], down[u][:], ALU.add)
+            nc.sync.dma_start(out_rows[:, u, :], res[u][:])
+            if u < 3:
+                nc.scalar.copy(out_in[:, :, u], res[u][:])
+            else:
+                nc.vector.tensor_copy(out_in[:, 0:352, u], res[u][:, 0:352])
+                nc.scalar.copy(out_in[:, 352:N, u], res[u][:, 352:N])
+
+        fetch_b(0)
+        fetch_b(1)
+        fetch_diff(0)
+        fetch_diff(1)
+        put_larger(0)
+        fetch_b(2)
+        put_smaller(0)
+        fetch_diff(2)
+        put_larger(1)
+        fetch_b(3)
+        put_smaller(1)
+        fetch_diff(3)
+        put_larger(2)
+        put_larger(3)
+        put_smaller(2)
+        put_smaller(3)
+
+        out_w = sb("out_w", [P, N], U32)
+        out_s = sb("out_s", [P, N], U8)
+        nc.vector.quantize_mx(out=out_w[:].bitcast(FP8X4), scales=out_s[:], in_=out_in[:].rearrange("p c t -> p (c t)"))
+        nc.sync.dma_start(out_1[0].rearrange("p n r -> p (n r)").bitcast(I32), out_w[:].bitcast(I32))
+        for q in range(4):
+            eng = nc.scalar if q % 2 == 0 else nc.sync
+            eng.dma_start(out_2[0, 4 * q : 4 * q + 4, :].bitcast(I32), out_s[32 * q : 32 * q + 4, :].bitcast(I32))

@@ -51,60 +51,68 @@ def tile_picked_kqtwicphoporder_none_po_kernel(
         nc.vector.memset(warm[:], 0.0)
         nc.vector.memset(w1s_raw[:].bitcast(I32), 0)
         gains = sb("gains", [P, 16], F32)
-        nc.gpsimd.dma_start(gains[:, 0:4], ga.rearrange("(p t) o -> p (t o)", t=4))
-        nc.gpsimd.dma_start(gains[:, 8:12], gb.rearrange("(p t) o -> p (t o)", t=4))
+        for col, src in ((8, gb), (0, ga)):
+            rows = src.rearrange("(g c) o -> g (c o)", c=8)
+            for e in range(2):
+                nc.gpsimd.dma_start(gains[e:P:2, col : col + 7], rows[:, e : e + 7])
 
         xw = sb("xw", [P, T], I32)
         w2w_raw = sb("w2w_raw", [P, 2 * N], U8)
         w1w_raw = sb("w1w_raw", [P, 2 * N], U8)
         l_two = load_list("l_two", two)
-        nc.scalar.dma_start(w2w_raw[:].bitcast(I32), w2_words[0].bitcast(I32))
-        nc.sync.dma_start(xw[:], x_words[0].rearrange("p n r -> p (n r)").bitcast(I32))
+        nc.sync.dma_start(w2w_raw[:].bitcast(I32), w2_words[0].bitcast(I32))
+        nc.sync.dma_start(w1w_raw[:].bitcast(I32), w1_words[0].bitcast(I32))
         load_scale_rows(xs, x_scales, nc.sync)
+        nc.sync.dma_start(xw[:], x_words[0].rearrange("p n r -> p (n r)").bitcast(I32))
         load_scale_rows(w2s_raw, w2_scales, nc.sync)
         nc.scalar.activation(warm_out[:], warm[:], ACT.Sigmoid)
         l_offs = load_list("l_offs", offs)
         l_n2 = load_list("l_n2", n2)
-        nc.sync.dma_start(w1w_raw[:].bitcast(I32), w1_words[0].bitcast(I32))
         load_scale_rows(w1s_raw, w1_scales, nc.sync)
         l_n1 = load_list("l_n1", n1)
         l_n3 = load_list("l_n3", n3)
         l_n5 = load_list("l_n5", n5)
         l_n4 = load_list("l_n4", n4)
 
-        step = sb("step", [P, 4], F32)
-        sign = sb("sign", [P, 4], F32)
+        flip = sb("flip", [P, 4], F32)
+        ga_neg = sb("ga_neg", [P, 4], F32)
         ga_abs = sb("ga_abs", [P, 4], F32)
-        gb_signed = sb("gb_signed", [P, 4], F32)
         gb_full = sb("gb_full", [P, 4], F32)
         gb_half = sb("gb_half", [P, 4], F32)
-        nc.gpsimd.tensor_scalar(step[:], gains[:, 0:4], 0.0, 2.0, ALU.is_ge, ALU.mult)
-        nc.gpsimd.tensor_scalar(sign[:], step[:], 1.0, -1.0, ALU.mult, ALU.add)
-        nc.gpsimd.tensor_tensor(gb_signed[:], gains[:, 8:12], sign[:], ALU.mult)
-        nc.gpsimd.tensor_scalar(gb_half[:], gb_signed[:], -0.5, 0.0, ALU.mult, ALU.add)
-        nc.gpsimd.tensor_scalar(gb_full[:], gb_signed[:], -1.0, 0.0, ALU.mult, ALU.add)
-        nc.gpsimd.tensor_tensor(ga_abs[:], gains[:, 0:4], sign[:], ALU.mult)
+        nc.gpsimd.tensor_scalar(flip[:], gains[:, 0:7:2], 0.0, -0.5, ALU.is_lt, ALU.add)
+        nc.gpsimd.tensor_tensor(gb_half[:], gains[:, 8:15:2], flip[:], ALU.mult)
+        nc.gpsimd.tensor_tensor(gb_full[:], gb_half[:], gb_half[:], ALU.add)
+        nc.gpsimd.tensor_tensor(ga_neg[:], gains[:, 0:7:2], flip[:], ALU.mult)
+        nc.gpsimd.tensor_scalar(ga_abs[:], ga_neg[:], -2.0, 0.0, ALU.mult, ALU.add)
 
-        def deal(name, raw, width, run):
-            dealt = sb(name, [P, width], U8)
+        def deal_words(name, raw):
+            dealt = sb(name, [P, 2 * N], U8)
             nc.vector.tensor_copy(
-                dealt[:].rearrange("p (t m r) -> p m t r", t=4, r=run),
-                raw[:].rearrange("p (m t r) -> p m t r", t=4, r=run),
+                dealt[:].bitcast(I32).rearrange("p (t g) -> p t g", t=4),
+                raw[:].bitcast(I32).rearrange("p (g t) -> p t g", t=4),
+            )
+            return dealt
+
+        def deal_scales(name, raw):
+            dealt = sb(name, [P, N], U8)
+            nc.vector.tensor_copy(
+                dealt[:].rearrange("p (t g e) -> p t g e", t=4, e=2),
+                raw[:].rearrange("p (g t e) -> p t g e", t=4, e=2),
             )
             return dealt
 
         xs_two = sb("xs_two", [P, N], U8)
         xs_offs = sb("xs_offs", [P, N], U8)
         xw_two = sb("xw_two", [P, N], U32)
-        w2w = deal("w2w", w2w_raw, 2 * N, 2)
+        w2w = deal_words("w2w", w2w_raw)
+        w1w = deal_words("w1w", w1w_raw)
         nc.vector.tensor_copy(xs_two[:], xs[:].indirect(l_two[:]))
         nc.vector.tensor_copy(xw_two[:], xw[:].bitcast(U32).indirect(l_two[:]))
-        w2s = deal("w2s", w2s_raw, N, 1)
+        w2s = deal_scales("w2s", w2s_raw)
         nc.vector.tensor_copy(xs_offs[:], xs[:].indirect(l_offs[:]))
         xw_offs = sb("xw_offs", [P, N], U32, tag="w2s_raw")
         nc.vector.tensor_copy(xw_offs[:], xw[:].bitcast(U32).indirect(l_offs[:]))
-        w1w = deal("w1w", w1w_raw, 2 * N, 2)
-        w1s = deal("w1s", w1s_raw, N, 1)
+        w1s = deal_scales("w1s", w1s_raw)
 
         def project(tag, ww, ws, words, scales, t):
             acc = psum.tile([P, N], F32, name=tag, tag=tag)
@@ -197,7 +205,7 @@ def tile_picked_kqtwicphoporder_none_po_kernel(
         down_abs = [sb("down_abs%d" % u, [P, HALF], F32) for u in range(4)]
         down = [sb("down%d" % u, [P, HALF], F32) for u in range(4)]
         res = [sb("res%d" % u, [P, N], F32) for u in range(4)]
-        out_in = sb("out_in", [P, N, 4], BF16)
+        out_in = [sb("out_in%d" % h, [P, HALF, 4], BF16) for h in range(2)]
         out_rows = out_0.rearrange("(p u) v -> p u v", u=4)
 
         def fetch_b(u):
@@ -215,11 +223,12 @@ def tile_picked_kqtwicphoporder_none_po_kernel(
         def put_smaller(u):
             nc.vector.tensor_tensor(res[u][:].indirect(l_n5[:]), pb[u][:], down[u][:], ALU.add)
             nc.sync.dma_start(out_rows[:, u, :], res[u][:])
-            if u < 3:
-                nc.scalar.copy(out_in[:, :, u], res[u][:])
-            else:
-                nc.vector.tensor_copy(out_in[:, 0:352, u], res[u][:, 0:352])
-                nc.scalar.copy(out_in[:, 352:N, u], res[u][:, 352:N])
+            for h in range(2):
+                cols = res[u][:, HALF * h : HALF * (h + 1)]
+                if u < 2 or h == 1:
+                    nc.scalar.copy(out_in[h][:, :, u], cols)
+                else:
+                    nc.vector.tensor_copy(out_in[h][:, :, u], cols)
 
         fetch_b(0)
         fetch_b(1)
@@ -240,8 +249,11 @@ def tile_picked_kqtwicphoporder_none_po_kernel(
 
         out_w = sb("out_w", [P, N], U32)
         out_s = sb("out_s", [P, N], U8)
-        nc.vector.quantize_mx(out=out_w[:].bitcast(FP8X4), scales=out_s[:], in_=out_in[:].rearrange("p c t -> p (c t)"))
-        nc.sync.dma_start(out_1[0].rearrange("p n r -> p (n r)").bitcast(I32), out_w[:].bitcast(I32))
+        words_out = out_1[0].rearrange("p n r -> p (n r)").bitcast(I32)
+        for h in range(2):
+            cols = slice(HALF * h, HALF * (h + 1))
+            nc.vector.quantize_mx(out=out_w[:, cols].bitcast(FP8X4), scales=out_s[:, cols], in_=out_in[h][:].rearrange("p c t -> p (c t)"))
+            nc.sync.dma_start(words_out[:, cols], out_w[:, cols].bitcast(I32))
         for q in range(4):
             eng = nc.scalar if q % 2 == 0 else nc.sync
             eng.dma_start(out_2[0, 4 * q : 4 * q + 4, :].bitcast(I32), out_s[32 * q : 32 * q + 4, :].bitcast(I32))

@@ -51,7 +51,7 @@ def tile_picked_kqtwicphoporder_none_po_kernel(
         nc.vector.memset(warm[:], 0.0)
         nc.vector.memset(w1s_raw[:].bitcast(I32), 0)
         gains = sb("gains", [P, 16], F32)
-        for col, src in ((8, gb), (0, ga)):
+        for col, src in ((0, ga), (8, gb)):
             rows = src.rearrange("(g c) o -> g (c o)", c=8)
             for e in range(2):
                 nc.gpsimd.dma_start(gains[e:P:2, col : col + 7], rows[:, e : e + 7])
@@ -60,14 +60,14 @@ def tile_picked_kqtwicphoporder_none_po_kernel(
         w2w_raw = sb("w2w_raw", [P, 2 * N], U8)
         w1w_raw = sb("w1w_raw", [P, 2 * N], U8)
         l_two = load_list("l_two", two)
+        l_offs = load_list("l_offs", offs)
         nc.sync.dma_start(w2w_raw[:].bitcast(I32), w2_words[0].bitcast(I32))
-        nc.sync.dma_start(w1w_raw[:].bitcast(I32), w1_words[0].bitcast(I32))
         load_scale_rows(xs, x_scales, nc.sync)
         nc.sync.dma_start(xw[:], x_words[0].rearrange("p n r -> p (n r)").bitcast(I32))
         load_scale_rows(w2s_raw, w2_scales, nc.sync)
         nc.scalar.activation(warm_out[:], warm[:], ACT.Sigmoid)
-        l_offs = load_list("l_offs", offs)
         l_n2 = load_list("l_n2", n2)
+        nc.sync.dma_start(w1w_raw[:].bitcast(I32), w1_words[0].bitcast(I32))
         load_scale_rows(w1s_raw, w1_scales, nc.sync)
         l_n1 = load_list("l_n1", n1)
         l_n3 = load_list("l_n3", n3)
@@ -76,14 +76,12 @@ def tile_picked_kqtwicphoporder_none_po_kernel(
 
         flip = sb("flip", [P, 4], F32)
         ga_neg = sb("ga_neg", [P, 4], F32)
-        ga_abs = sb("ga_abs", [P, 4], F32)
         gb_full = sb("gb_full", [P, 4], F32)
         gb_half = sb("gb_half", [P, 4], F32)
         nc.gpsimd.tensor_scalar(flip[:], gains[:, 0:7:2], 0.0, -0.5, ALU.is_lt, ALU.add)
         nc.gpsimd.tensor_tensor(gb_half[:], gains[:, 8:15:2], flip[:], ALU.mult)
         nc.gpsimd.tensor_tensor(gb_full[:], gb_half[:], gb_half[:], ALU.add)
         nc.gpsimd.tensor_tensor(ga_neg[:], gains[:, 0:7:2], flip[:], ALU.mult)
-        nc.gpsimd.tensor_scalar(ga_abs[:], ga_neg[:], -2.0, 0.0, ALU.mult, ALU.add)
 
         def deal_words(name, raw):
             dealt = sb(name, [P, 2 * N], U8)
@@ -105,13 +103,13 @@ def tile_picked_kqtwicphoporder_none_po_kernel(
         xs_offs = sb("xs_offs", [P, N], U8)
         xw_two = sb("xw_two", [P, N], U32)
         w2w = deal_words("w2w", w2w_raw)
-        w1w = deal_words("w1w", w1w_raw)
         nc.vector.tensor_copy(xs_two[:], xs[:].indirect(l_two[:]))
+        nc.vector.tensor_copy(xs_offs[:], xs[:].indirect(l_offs[:]))
         nc.vector.tensor_copy(xw_two[:], xw[:].bitcast(U32).indirect(l_two[:]))
         w2s = deal_scales("w2s", w2s_raw)
-        nc.vector.tensor_copy(xs_offs[:], xs[:].indirect(l_offs[:]))
         xw_offs = sb("xw_offs", [P, N], U32, tag="w2s_raw")
         nc.vector.tensor_copy(xw_offs[:], xw[:].bitcast(U32).indirect(l_offs[:]))
+        w1w = deal_words("w1w", w1w_raw)
         w1s = deal_scales("w1s", w1s_raw)
 
         def project(tag, ww, ws, words, scales, t):
@@ -149,6 +147,8 @@ def tile_picked_kqtwicphoporder_none_po_kernel(
             sg = sb("sig%d" % t, [P, N], F32)
             nc.scalar.activation(sg[:], a_win[:].indirect(l_n1[:]), ACT.Sigmoid)
             sig.append(sg)
+        ga_abs = sb("ga_abs", [P, 4], F32, tag="a_win1")
+        nc.gpsimd.tensor_scalar(ga_abs[:], ga_neg[:], -2.0, 0.0, ALU.mult, ALU.add)
         z2 = sb("z2", [P, 4, N], F32)
         for t in range(4):
             nc.vector.tensor_tensor(z2[:, t, :], st2[t][:].indirect(l_n3[:]), st2_copy[t][:], ALU.subtract)
@@ -168,22 +168,33 @@ def tile_picked_kqtwicphoporder_none_po_kernel(
         def larger(t):
             nc.vector.tensor_tensor(z[:, t, :], st[t][:, 0:N], st_n1[t][:], ALU.max)
 
-        for stage in (gate, fetch):
-            for t in range(4):
-                stage(t)
+        for step in range(6):
+            if step < 4:
+                gate(step)
+            if step >= 3:
+                larger(step - 3)
+            if 1 <= step <= 4:
+                fetch(step - 1)
         z2_w = sb("z2_w", [P, N], U32)
         z2_s = sb("z2_s", [P, N], U8)
+        larger(3)
         nc.vector.quantize_mx(out=z2_w[:].bitcast(FP8X4), scales=z2_s[:], in_=z2_in[:].rearrange("p c t -> p (c t)"))
-        for t in range(4):
-            larger(t)
 
         z_in = [sb("z_in%d" % u, [P, P, 4], BF16) for u in range(4)]
         z_w = [sb("z_w%d" % u, [P, P], U32) for u in range(4)]
         z_s = [sb("z_s%d" % u, [P, P], U8) for u in range(4)]
         s_win = [sb("s_win%d" % u, [P, N], F32) for u in range(4)]
 
+        sixteenth = [sb("sixteenth%d" % u, [P, 1], F32) for u in range(4)]
+        for u in range(4):
+            nc.gpsimd.memset(sixteenth[u][:], 0.0625)
+
         def weave(u):
-            nc.vector.tensor_copy(z_in[u][:], z[:].rearrange("p t (m u) -> p u m t", u=4)[:, u])
+            src = z[:].rearrange("p t (m u) -> p u m t", u=4)[:, u]
+            if u < 3:
+                nc.vector.tensor_copy(z_in[u][:], src)
+            else:
+                nc.scalar.copy(z_in[u][:], src)
 
         def product(u):
             nc.vector.quantize_mx(out=z_w[u][:].bitcast(FP8X4), scales=z_s[u][:], in_=z_in[u][:].rearrange("p m t -> p (m t)"))
@@ -191,7 +202,7 @@ def tile_picked_kqtwicphoporder_none_po_kernel(
             nc.tensor.matmul_mx(
                 out=acc[:], lhsT=z_w[u][:].bitcast(FP8X4), lhsT_scale=z_s[u][:], rhs=z2_w[:].bitcast(FP8X4), rhs_scale=z2_s[:], start=True, stop=True
             )
-            nc.scalar.activation(s_win[u][:], acc[:], ACT.Copy, scale=0.0625)
+            nc.scalar.activation(s_win[u][:], acc[:], ACT.Copy, scale=sixteenth[u][:])
 
         weave(0)
         for u in range(4):
@@ -200,7 +211,7 @@ def tile_picked_kqtwicphoporder_none_po_kernel(
             product(u)
 
         pb = [sb("pb%d" % u, [P, HALF], F32) for u in range(4)]
-        diff = [sb("diff%d" % u, [P, HALF], F32) for u in range(4)]
+        diff = [sb("diff%d" % u, [P, HALF], F32, tag="sixteenth%d" % min(u + 1, 3) if u < 3 else None) for u in range(4)]
         up = [sb("up%d" % u, [P, HALF], F32) for u in range(4)]
         down_abs = [sb("down_abs%d" % u, [P, HALF], F32) for u in range(4)]
         down = [sb("down%d" % u, [P, HALF], F32) for u in range(4)]
@@ -213,7 +224,11 @@ def tile_picked_kqtwicphoporder_none_po_kernel(
 
         def fetch_diff(u):
             nc.vector.tensor_tensor(diff[u][:], s_win[u][:].indirect(l_n4[:]), pb[u][:], ALU.subtract)
+
+        def part_up(u):
             nc.scalar.activation(up[u][:], diff[u][:], ACT.Relu)
+
+        def part_down(u):
             nc.scalar.activation(down_abs[u][:], diff[u][:], ACT.Relu, scale=-1.0)
             nc.scalar.activation(down[u][:], down_abs[u][:], ACT.Copy, scale=-1.0)
 
@@ -223,6 +238,8 @@ def tile_picked_kqtwicphoporder_none_po_kernel(
         def put_smaller(u):
             nc.vector.tensor_tensor(res[u][:].indirect(l_n5[:]), pb[u][:], down[u][:], ALU.add)
             nc.sync.dma_start(out_rows[:, u, :], res[u][:])
+
+        def round_rows(u):
             for h in range(2):
                 cols = res[u][:, HALF * h : HALF * (h + 1)]
                 if u < 2 or h == 1:
@@ -230,27 +247,28 @@ def tile_picked_kqtwicphoporder_none_po_kernel(
                 else:
                     nc.vector.tensor_copy(out_in[h][:, :, u], cols)
 
-        fetch_b(0)
-        fetch_b(1)
-        fetch_diff(0)
-        fetch_diff(1)
-        put_larger(0)
-        fetch_b(2)
-        put_smaller(0)
-        fetch_diff(2)
-        put_larger(1)
-        fetch_b(3)
-        put_smaller(1)
-        fetch_diff(3)
-        put_larger(2)
-        put_larger(3)
-        put_smaller(2)
-        put_smaller(3)
+        for step in range(5):
+            if step < 4:
+                fetch_b(step)
+            if step > 0:
+                fetch_diff(step - 1)
+        for step in range(5):
+            if step < 4:
+                part_up(step)
+            if step > 0:
+                part_down(step - 1)
+        for step in range(5):
+            if step < 4:
+                put_larger(step)
+            if step > 0:
+                put_smaller(step - 1)
+        for u in range(4):
+            round_rows(u)
 
         out_w = sb("out_w", [P, N], U32)
         out_s = sb("out_s", [P, N], U8)
         words_out = out_1[0].rearrange("p n r -> p (n r)").bitcast(I32)
-        for h in range(2):
+        for h in (1, 0):
             cols = slice(HALF * h, HALF * (h + 1))
             nc.vector.quantize_mx(out=out_w[:, cols].bitcast(FP8X4), scales=out_s[:, cols], in_=out_in[h][:].rearrange("p c t -> p (c t)"))
             nc.sync.dma_start(words_out[:, cols], out_w[:, cols].bitcast(I32))

from contextlib import ExitStack

import concourse.mybir as mybir

F32 = mybir.dt.float32
BF16 = mybir.dt.bfloat16
I32 = mybir.dt.int32
U32 = mybir.dt.uint32
U16 = mybir.dt.uint16
U8 = mybir.dt.uint8
FP8X4 = mybir.dt.float8_e4m3fn_x4
FP4X4 = mybir.dt.float4_e2m1fn_x4
ALU = mybir.AluOpType
ACT = mybir.ActivationFunctionType

P = 128
T = 2048
N = 512
HALF = 256
WIN = 1024
FLOPS = 3 * 2 * 512 * 512 * 512


def tile_picked_kqtwicphoporder_none_po_kernel(
    tc, x_words, x_scales, w1_words, w1_scales, w2_words, w2_scales, ga, gb, offs, two, n1, n2, n3, n4, n5, out_0, out_1, out_2
):
    nc = tc.nc
    with ExitStack() as ctx:
        keep = ctx.enter_context(tc.tile_pool(name="keep", bufs=1))
        psum = ctx.enter_context(tc.psum_pool(name="psum", bufs=1))

        def sb(name, shape, dtype, tag=None):
            return keep.tile(shape, dtype, name=name, tag=tag or name, align_bytes=64)

        def load_list(name, src):
            lst = keep.tile(list(src.shape), U16, name=name)
            nc.sync.dma_start(lst[:], src)
            return lst

        def load_scale_rows(tile, src, queue):
            for q in range(4):
                queue.dma_start(tile[32 * q : 32 * q + 4, :].bitcast(I32), src[0, 4 * q : 4 * q + 4, :].bitcast(I32))

        xs = sb("xs", [P, T], U8)
        w2s_raw = sb("w2s_raw", [P, N], U8)
        w1s_raw = sb("w1s_raw", [P, N], U8)
        warm = sb("warm", [P, 8], F32)
        warm_out = sb("warm_out", [P, 8], F32)
        nc.gpsimd.memset(xs[:].bitcast(I32), 0)
        nc.vector.memset(w2s_raw[:].bitcast(I32), 0)
        nc.vector.memset(warm[:], 0.0)
        nc.vector.memset(w1s_raw[:].bitcast(I32), 0)
        gains = sb("gains", [P, 16], F32)
        for col, src in ((0, ga), (8, gb)):
            rows = src.rearrange("(g c) o -> g (c o)", c=8)
            for e in range(2):
                nc.gpsimd.dma_start(gains[e:P:2, col : col + 7], rows[:, e : e + 7])

        xw = sb("xw", [P, T], I32)
        w2w_raw = sb("w2w_raw", [P, 2 * N], U8)
        w1w_raw = sb("w1w_raw", [P, 2 * N], U8)
        l_two = load_list("l_two", two)
        l_offs = load_list("l_offs", offs)
        nc.sync.dma_start(w2w_raw[:].bitcast(I32), w2_words[0].bitcast(I32))
        load_scale_rows(xs, x_scales, nc.sync)
        nc.sync.dma_start(xw[:], x_words[0].rearrange("p n r -> p (n r)").bitcast(I32))
        load_scale_rows(w2s_raw, w2_scales, nc.sync)
        nc.scalar.activation(warm_out[:], warm[:], ACT.Sigmoid)
        l_n2 = load_list("l_n2", n2)
        nc.sync.dma_start(w1w_raw[:].bitcast(I32), w1_words[0].bitcast(I32))
        load_scale_rows(w1s_raw, w1_scales, nc.sync)
        l_n1 = load_list("l_n1", n1)
        l_n3 = load_list("l_n3", n3)
        l_n5 = load_list("l_n5", n5)
        l_n4 = load_list("l_n4", n4)

        flip = sb("flip", [P, 4], F32)
        ga_neg = sb("ga_neg", [P, 4], F32)
        gb_full = sb("gb_full", [P, 4], F32)
        gb_half = sb("gb_half", [P, 4], F32)
        nc.gpsimd.tensor_scalar(flip[:], gains[:, 0:7:2], 0.0, -0.5, ALU.is_lt, ALU.add)
        nc.gpsimd.tensor_tensor(gb_half[:], gains[:, 8:15:2], flip[:], ALU.mult)
        nc.gpsimd.tensor_tensor(gb_full[:], gb_half[:], gb_half[:], ALU.add)
        nc.gpsimd.tensor_tensor(ga_neg[:], gains[:, 0:7:2], flip[:], ALU.mult)

        def deal_words(name, raw):
            dealt = sb(name, [P, 2 * N], U8)
            nc.vector.tensor_copy(
                dealt[:].bitcast(I32).rearrange("p (t g) -> p t g", t=4),
                raw[:].bitcast(I32).rearrange("p (g t) -> p t g", t=4),
            )
            return dealt

        def deal_scales(name, raw):
            dealt = sb(name, [P, N], U8)
            nc.vector.tensor_copy(
                dealt[:].rearrange("p (t g e) -> p t g e", t=4, e=2),
                raw[:].rearrange("p (g t e) -> p t g e", t=4, e=2),
            )
            return dealt

        xs_two = sb("xs_two", [P, N], U8)
        xs_offs = sb("xs_offs", [P, N], U8)
        xw_two = sb("xw_two", [P, N], U32)
        w2w = deal_words("w2w", w2w_raw)
        nc.vector.tensor_copy(xs_two[:], xs[:].indirect(l_two[:]))
        nc.vector.tensor_copy(xs_offs[:], xs[:].indirect(l_offs[:]))
        nc.vector.tensor_copy(xw_two[:], xw[:].bitcast(U32).indirect(l_two[:]))
        w2s = deal_scales("w2s", w2s_raw)
        xw_offs = sb("xw_offs", [P, N], U32, tag="w2s_raw")
        nc.vector.tensor_copy(xw_offs[:], xw[:].bitcast(U32).indirect(l_offs[:]))
        w1w = deal_words("w1w", w1w_raw)
        w1s = deal_scales("w1s", w1s_raw)

        def project(tag, ww, ws, words, scales, t):
            acc = psum.tile([P, N], F32, name=tag, tag=tag)
            nc.tensor.matmul_mx(
                out=acc[:],
                lhsT=ww[:, 2 * P * t : 2 * P * (t + 1)].bitcast(FP4X4),
                lhsT_scale=ws[:, P * t : P * (t + 1)],
                rhs=words[:].bitcast(FP8X4),
                rhs_scale=scales[:],
                start=True,
                stop=True,
            )
            return acc

        b_ps = [project("b%d" % t, w2w, w2s, xw_two, xs_two, t) for t in range(4)]
        a_ps = [project("a%d" % t, w1w, w1s, xw_offs, xs_offs, t) for t in range(4)]
        st2 = []
        st2_copy = []
        for t in range(4):
            half_win = sb("half_win%d" % t, [P, WIN], F32)
            b_full = sb("b_full%d" % t, [P, N], F32)
            nc.scalar.activation(half_win[:, 0:N], b_ps[t][:], ACT.Copy, scale=gb_half[:, t : t + 1])
            nc.scalar.activation(b_full[:], b_ps[t][:], ACT.Copy, scale=gb_full[:, t : t + 1])
            win = sb("st2_%d" % t, [P, WIN], F32)
            nc.vector.tensor_tensor(win[:, 0:N], half_win[:].indirect(l_n2[:]), b_full[:], ALU.add)
            cp = sb("st2_copy%d" % t, [P, N], F32)
            nc.sync.dma_start(cp[:], win[:, 0:N])
            st2.append(win)
            st2_copy.append(cp)
        sig = []
        for t in range(4):
            a_win = sb("a_win%d" % t, [P, WIN], F32)
            nc.scalar.copy(a_win[:, 0:N], a_ps[t][:])
            sg = sb("sig%d" % t, [P, N], F32)
            nc.scalar.activation(sg[:], a_win[:].indirect(l_n1[:]), ACT.Sigmoid)
            sig.append(sg)
        ga_abs = sb("ga_abs", [P, 4], F32, tag="a_win1")
        nc.gpsimd.tensor_scalar(ga_abs[:], ga_neg[:], -2.0, 0.0, ALU.mult, ALU.add)
        z2 = sb("z2", [P, 4, N], F32)
        for t in range(4):
            nc.vector.tensor_tensor(z2[:, t, :], st2[t][:].indirect(l_n3[:]), st2_copy[t][:], ALU.subtract)
        z2_in = sb("z2_in", [P, N, 4], BF16)
        nc.scalar.copy(z2_in[:], z2[:].rearrange("p t c -> p c t"))

        st = [sb("st%d" % t, [P, WIN], F32) for t in range(4)]
        st_n1 = [sb("st_n1_%d" % t, [P, N], F32) for t in range(4)]
        z = sb("z", [P, 4, N], BF16)

        def gate(t):
            nc.vector.scalar_tensor_tensor(st[t][:, 0:N], a_ps[t][:], ga_abs[:, t : t + 1], sig[t][:], ALU.mult, ALU.mult)

        def fetch(t):
            nc.vector.tensor_copy(st_n1[t][:], st[t][:].indirect(l_n1[:]))

        def larger(t):
            nc.vector.tensor_tensor(z[:, t, :], st[t][:, 0:N], st_n1[t][:], ALU.max)

        for step in range(6):
            if step < 4:
                gate(step)
            if step >= 3:
                larger(step - 3)
            if 1 <= step <= 4:
                fetch(step - 1)
        z2_w = sb("z2_w", [P, N], U32)
        z2_s = sb("z2_s", [P, N], U8)
        larger(3)
        nc.vector.quantize_mx(out=z2_w[:].bitcast(FP8X4), scales=z2_s[:], in_=z2_in[:].rearrange("p c t -> p (c t)"))

        z_in = [sb("z_in%d" % u, [P, P, 4], BF16) for u in range(4)]
        z_w = [sb("z_w%d" % u, [P, P], U32) for u in range(4)]
        z_s = [sb("z_s%d" % u, [P, P], U8) for u in range(4)]
        s_win = [sb("s_win%d" % u, [P, N], F32) for u in range(4)]

        sixteenth = [sb("sixteenth%d" % u, [P, 1], F32) for u in range(4)]
        for u in range(4):
            nc.gpsimd.memset(sixteenth[u][:], 0.0625)

        def weave(u):
            src = z[:].rearrange("p t (m u) -> p u m t", u=4)[:, u]
            if u < 3:
                nc.vector.tensor_copy(z_in[u][:], src)
            else:
                nc.scalar.copy(z_in[u][:], src)

        def product(u):
            nc.vector.quantize_mx(out=z_w[u][:].bitcast(FP8X4), scales=z_s[u][:], in_=z_in[u][:].rearrange("p m t -> p (m t)"))
            acc = psum.tile([P, N], F32, name="s%d" % u, tag="b%d" % u)
            nc.tensor.matmul_mx(
                out=acc[:], lhsT=z_w[u][:].bitcast(FP8X4), lhsT_scale=z_s[u][:], rhs=z2_w[:].bitcast(FP8X4), rhs_scale=z2_s[:], start=True, stop=True
            )
            nc.scalar.activation(s_win[u][:], acc[:], ACT.Copy, scale=sixteenth[u][:])

        weave(0)
        for u in range(4):
            if u + 1 < 4:
                weave(u + 1)
            product(u)

        pb = [sb("pb%d" % u, [P, HALF], F32) for u in range(4)]
        diff = [sb("diff%d" % u, [P, HALF], F32, tag="sixteenth%d" % min(u + 1, 3) if u < 3 else None) for u in range(4)]
        up = [sb("up%d" % u, [P, HALF], F32) for u in range(4)]
        down_abs = [sb("down_abs%d" % u, [P, HALF], F32) for u in range(4)]
        down = [sb("down%d" % u, [P, HALF], F32) for u in range(4)]
        res = [sb("res%d" % u, [P, N], F32) for u in range(4)]
        out_in = [sb("out_in%d" % h, [P, HALF, 4], BF16) for h in range(2)]
        out_rows = out_0.rearrange("(p u) v -> p u v", u=4)

        def fetch_b(u):
            nc.vector.tensor_copy(pb[u][:], s_win[u][:].indirect(l_n5[:]))

        def fetch_diff(u):
            nc.vector.tensor_tensor(diff[u][:], s_win[u][:].indirect(l_n4[:]), pb[u][:], ALU.subtract)

        def part_up(u):
            nc.scalar.activation(up[u][:], diff[u][:], ACT.Relu)

        def part_down(u):
            nc.scalar.activation(down_abs[u][:], diff[u][:], ACT.Relu, scale=-1.0)
            nc.scalar.activation(down[u][:], down_abs[u][:], ACT.Copy, scale=-1.0)

        def put_larger(u):
            nc.vector.tensor_tensor(res[u][:].indirect(l_n4[:]), pb[u][:], up[u][:], ALU.add)

        def put_smaller(u):
            nc.vector.tensor_tensor(res[u][:].indirect(l_n5[:]), pb[u][:], down[u][:], ALU.add)
            nc.sync.dma_start(out_rows[:, u, :], res[u][:])

        def round_rows(u):
            for h in range(2):
                cols = res[u][:, HALF * h : HALF * (h + 1)]
                if u < 2 or h == 1:
                    nc.scalar.copy(out_in[h][:, :, u], cols)
                else:
                    nc.vector.tensor_copy(out_in[h][:, :, u], cols)

        for step in range(5):
            if step < 4:
                fetch_b(step)
            if step > 0:
                fetch_diff(step - 1)
        for step in range(5):
            if step < 4:
                part_up(step)
            if step > 0:
                part_down(step - 1)
        for step in range(5):
            if step < 4:
                put_larger(step)
            if step > 0:
                put_smaller(step - 1)
        for u in range(4):
            round_rows(u)

        out_w = sb("out_w", [P, N], U32)
        out_s = sb("out_s", [P, N], U8)
        words_out = out_1[0].rearrange("p n r -> p (n r)").bitcast(I32)
        for h in (1, 0):
            cols = slice(HALF * h, HALF * (h + 1))
            nc.vector.quantize_mx(out=out_w[:, cols].bitcast(FP8X4), scales=out_s[:, cols], in_=out_in[h][:].rearrange("p c t -> p (c t)"))
            nc.sync.dma_start(words_out[:, cols], out_w[:, cols].bitcast(I32))
        for q in range(4):
            eng = nc.scalar if q % 2 == 0 else nc.sync
            eng.dma_start(out_2[0, 4 * q : 4 * q + 4, :].bitcast(I32), out_s[32 * q : 32 * q + 4, :].bitcast(I32))
